import numpy as np
import ml_dtypes


def mxq(x, axis, fmt="e4m3"):
    dtype, down = {"e4m3": (ml_dtypes.float8_e4m3fn, 7), "e5m2": (ml_dtypes.float8_e5m2, 14)}[fmt]
    v = np.moveaxis(np.asarray(x, np.float32).astype(ml_dtypes.bfloat16).astype(np.float64), axis, -1)
    blocks = v.reshape(v.shape[:-1] + (-1, 32))
    amax = np.abs(blocks).max(-1, keepdims=True)
    byte = np.maximum(np.where(amax > 0, np.frexp(amax)[1] - 1 + 127, 0) - down, 1)
    scale = np.exp2(byte - 127.0)
    codes = (blocks / scale).astype(np.float32).astype(dtype).astype(np.float64)
    return np.moveaxis((codes * scale).reshape(v.shape), -1, axis)


WIDE = False


def mx_kscale(k):
    if not WIDE:
        return np.ones(k)
    levels = np.array([10, -10, 5, -5, 0])
    if k % 512:
        return np.exp2(np.random.permutation(np.resize(levels, k // 32))).repeat(32)
    a = np.empty((k // 512, 16))
    for p in range(k // 512):
        a[p, :8] = np.random.permutation(np.resize(levels, 8))
        for g in range(8):
            far = levels[np.abs(levels - a[p, g]) >= 10]
            a[p, g + 8] = far[np.random.randint(len(far))]
    return np.exp2(a.ravel()).repeat(32)


def f64(x):
    return np.asarray(x).astype(np.float64)


def striped(idx):
    return np.tile(idx.reshape(-1, 16).T, (8, 1)).astype(np.uint16)


def unstriped(offs):
    return offs[:16].T.reshape(-1).astype(np.int64)


def striped8(idx):
    return np.concatenate([x.reshape(-1, 16).T for x in idx]).astype(np.uint16)


def runs(offs, k):
    lists = np.stack([offs[16 * r : 16 * r + 16].T.reshape(-1) for r in range(8)]).astype(np.int64)
    return lists[np.arange(k) % 512 // 64]


def pack_weight(w):
    k, n = w.shape
    w = f64(np.asarray(w, np.float32).astype(ml_dtypes.bfloat16)).reshape(k // 32, 32, n)
    amax = np.abs(w).max(1)
    byte = np.clip(np.where(amax > 0, np.frexp(amax)[1] - 1 + 127 - 7, 1), 1, 254)
    scaled = (w * np.exp2(127.0 - byte)[:, None, :]).reshape(k, n).astype(np.float32)
    words = np.ascontiguousarray(scaled.reshape(k // 512, 128, 4, n).transpose(0, 1, 3, 2)).astype(ml_dtypes.float8_e4m3fn).view(np.uint8)
    return words, np.ascontiguousarray(byte.astype(np.uint8).reshape(k // 512, 16, n))


def unpack_weight(words, scales):
    g, p, n, _ = words.shape
    vals = np.ascontiguousarray(words).view(ml_dtypes.float8_e4m3fn).astype(np.float64) * np.repeat(np.exp2(scales.astype(np.float64) - 127.0), 8, axis=1)[..., None]
    return vals.transpose(0, 1, 3, 2).reshape(g * 512, n)


def sigmoid(v):
    return 1.0 / (1.0 + np.exp(-np.maximum(v, -700.0)))


K, T, S, H, G = 512, 2048, 512, 512, 2048


def setup_inputs():
    n = np.random.standard_normal
    s = mx_kscale(K)[:, None]
    packed_xT = pack_weight(n((K, T)) * s)
    packed_dT = pack_weight(n((K, G)) / s)
    return {
        "x_words": packed_xT[0],
        "x_scales": packed_xT[1],
        "w1": (n((K, H)) / np.sqrt(K) / s).astype(np.float32),
        "gs": (np.random.uniform(0.5, 1.5, (K, 1)) * s).astype(np.float32),
        "d_words": packed_dT[0],
        "d_scales": packed_dT[1],
        "offs": striped(np.random.permutation(T)[:S]),
        "n1": striped8(np.stack([np.random.permutation(S) for _ in range(8)])),
        "n2": striped8(np.stack([np.random.permutation(S) for _ in range(8)])),
        "n3": striped8(np.stack([np.random.permutation(S) for _ in range(8)])),
        "k1": striped8(np.random.randint(0, G, (8, H))),
        "n4": striped8(np.stack([np.random.permutation(S) for _ in range(8)])),
        "n5": striped8(np.stack([np.random.permutation(S) for _ in range(8)])),
    }


def reference(x_words, x_scales, w1, gs, d_words, d_scales, offs, n1, n2, n3, k1, n4, n5):
    d_k1 = unpack_weight(d_words, d_scales)[np.arange(K)[:, None], runs(k1, K)]
    xq = unpack_weight(x_words, x_scales)[:, unstriped(offs)]
    y = mxq(f64(w1), 0, "e4m3").T @ xq
    z = f64(gs) * (0.75 * (y * (y[np.arange(H)[:, None], runs(n1, H)]) + (y[np.arange(H)[:, None], runs(n2, H)]) * (y[np.arange(H)[:, None], runs(n3, H)])))
    h = 0.0625 * ((d_k1.T @ mxq(z, 0, "e4m3")))
    st = h * (sigmoid(h[np.arange(H)[:, None], runs(n4, H)]))
    return st - (st[np.arange(H)[:, None], runs(n5, H)])

@@ -1,0 +1,182 @@
+from contextlib import ExitStack
+
+import concourse.mybir as mybir
+
+K, T, S, H, G = 512, 2048, 512, 512, 2048
+FLOPS = 2 * K * H * S * 2
+
+F32 = mybir.dt.float32
+BF16 = mybir.dt.bfloat16
+I32 = mybir.dt.int32
+U32 = mybir.dt.uint32
+U16 = mybir.dt.uint16
+U8 = mybir.dt.uint8
+FP8X4 = mybir.dt.float8_e4m3fn_x4
+ACT = mybir.ActivationFunctionType
+ALU = mybir.AluOpType
+
+P = 128
+PACK = 4
+HALF = S // 2
+
+
+def tile_picked_densedothopg_none_p_kernel(tc, x_words, x_scales, w1, gs, d_words, d_scales, offs, n1, n2, n3, k1, n4, n5, out):
+    nc = tc.nc
+    with ExitStack() as ctx:
+        lists = ctx.enter_context(tc.tile_pool(name="lists", bufs=1))
+        sb = ctx.enter_context(tc.tile_pool(name="sb", bufs=1))
+        psum = ctx.enter_context(tc.psum_pool(name="psum", bufs=1))
+
+        def load_list(src, name):
+            tile = lists.tile([P, S // 16], U16, name=name)
+            nc.sync.dma_start(tile[:], src)
+            return tile
+
+        def gather(eng, dst, window, lst, h, scale=None, bias=None):
+            src = window[:].indirect(lst[:, h * (HALF // 16) : (h + 1) * (HALF // 16)])
+            if eng == "v":
+                if scale is None:
+                    nc.vector.tensor_copy(dst, src)
+                else:
+                    nc.vector.tensor_scalar(dst, src, scale, bias, ALU.mult, ALU.add)
+            else:
+                if scale is None:
+                    nc.scalar.activation(dst, src, ACT.Copy)
+                else:
+                    nc.scalar.activation(dst, src, ACT.Copy, bias=bias, scale=scale)
+
+        xs_win = sb.tile([P, T], U8, name="xs_win")
+        ds_win = sb.tile([P, G], U8, name="ds_win")
+        nc.gpsimd.memset(xs_win[:].bitcast(I32), 0)
+        nc.vector.memset(ds_win[:].bitcast(I32), 0)
+        offs_t = load_list(offs, "offs_t")
+        k1_t = load_list(k1, "k1_t")
+        w_rows = w1.rearrange("(p j) c -> p j c", j=PACK)
+        w_raw = [sb.tile([P, PACK, H // 2], F32, name=f"w_raw{a}") for a in range(2)]
+        nc.sync.dma_start(w_raw[0][:], w_rows[:, :, 0 : H // 2])
+        for q in range(4):
+            nc.gpsimd.dma_start(xs_win[32 * q : 32 * q + 4, :].bitcast(I32), x_scales[0][4 * q : 4 * q + 4, :].bitcast(I32))
+        n1_t = load_list(n1, "n1_t")
+        n2_t = load_list(n2, "n2_t")
+        nc.sync.dma_start(w_raw[1][:], w_rows[:, :, H // 2 : H])
+        xw_win = sb.tile([P, T], I32, name="xw_win")
+        nc.sync.dma_start(xw_win[:], x_words[0].rearrange("p n t -> p (n t)").bitcast(I32))
+        for r in range(2):
+            nc.scalar.dma_start(ds_win[r:P:16, :].bitcast(I32), d_scales[0][r:16:2, :].bitcast(I32))
+        gs_t = sb.tile([P, PACK], F32, name="gs_t")
+        nc.gpsimd.dma_start(gs_t[:], gs.rearrange("(p t) o -> p (t o)", t=PACK))
+        n3_t = load_list(n3, "n3_t")
+        dw_win = sb.tile([P, G], I32, name="dw_win")
+        nc.sync.dma_start(dw_win[:], d_words[0].rearrange("p n t -> p (n t)").bitcast(I32))
+        n4_t = load_list(n4, "n4_t")
+        n5_t = load_list(n5, "n5_t")
+        coef = sb.tile([P, PACK], F32, name="coef")
+        nc.gpsimd.tensor_scalar(coef[:], gs_t[:], 0.75, 0.0, ALU.mult, ALU.add)
+
+        xs_g = sb.tile([P, S], U8, name="xs_g", align_bytes=64)
+        nc.vector.tensor_copy(xs_g[:], xs_win[:].indirect(offs_t[:]))
+        ds_g = sb.tile([P, H], U8, name="ds_g", align_bytes=64)
+        nc.vector.tensor_copy(ds_g[:], ds_win[:].indirect(k1_t[:]))
+        ds_dealt = sb.tile([P, H], U8, name="ds_dealt", align_bytes=64)
+        nc.vector.tensor_copy(
+            ds_dealt[:].rearrange("p (t c i) -> p c t i", t=PACK, i=16),
+            ds_g[:].rearrange("p (c i t) -> p c t i", t=PACK, i=16),
+        )
+        for r in range(2):
+            nc.sync.dma_start(ds_dealt[2 + r : P : 32, :].bitcast(I32), ds_dealt[16 + r : P : 32, :].bitcast(I32))
+
+        w_bf = sb.tile([P, PACK * H], BF16, name="w_bf", align_bytes=64)
+        w_view = w_bf[:].rearrange("p (t m j) -> p m t j", t=PACK, j=PACK)
+        for a in range(2):
+            nc.scalar.activation(w_view[:, 64 * a : 64 * (a + 1)], w_raw[a][:].rearrange("p j (m t) -> p m t j", t=PACK), ACT.Copy)
+        w_codes = sb.tile([P, H], U32, name="w_codes", align_bytes=64)
+        w_scales = sb.tile([P, H], U8, name="w_scales", align_bytes=64)
+        nc.vector.quantize_mx(out=w_codes[:].bitcast(FP8X4), scales=w_scales[:], in_=w_bf[:])
+
+        y_ps = [[psum.tile([P, 2, HALF], F32, name=f"y_ps{h}{u}") for u in range(2)] for h in range(2)]
+        y_win = [sb.tile([P, S], F32, name=f"y_win{t}") for t in range(PACK)]
+        for h in range(2):
+            xw_g = sb.tile([P, HALF], U32, name=f"xw_g{h}", align_bytes=64)
+            nc.vector.tensor_copy(xw_g[:], xw_win[:].bitcast(U32).indirect(offs_t[:, 16 * h : 16 * (h + 1)]))
+            for t in range(PACK):
+                nc.tensor.matmul_mx(
+                    out=y_ps[h][t // 2][:, t % 2, :],
+                    lhsT=w_codes[:, P * t : P * (t + 1)].bitcast(FP8X4),
+                    lhsT_scale=w_scales[:, P * t : P * (t + 1)],
+                    rhs=xw_g[:].bitcast(FP8X4),
+                    rhs_scale=xs_g[:, HALF * h : HALF * (h + 1)],
+                    start=True,
+                    stop=True,
+                )
+            for t in range(PACK):
+                nc.scalar.activation(y_win[t][:, HALF * h : HALF * (h + 1)], y_ps[h][t // 2][:, t % 2, :], ACT.Copy)
+
+        dw_g = sb.tile([P, H], U32, name="dw_g", align_bytes=64)
+        nc.vector.tensor_copy(dw_g[:], dw_win[:].bitcast(U32).indirect(k1_t[:]))
+        dw_dealt = sb.tile([P, H], U32, name="dw_dealt", align_bytes=64)
+        nc.vector.tensor_copy(
+            dw_dealt[:].rearrange("p (t c i) -> p c t i", t=PACK, i=4),
+            dw_g[:].rearrange("p (c i t) -> p c t i", t=PACK, i=4),
+        )
+
+        h_ps = [[psum.tile([P, 2, HALF], F32, name=f"h_ps{h}{u}") for u in range(2)] for h in range(2)]
+        th_win = [sb.tile([P, S], F32, name=f"th_win{t}") for t in range(PACK)]
+        for h in range(2):
+            g1 = sb.tile([P, PACK, HALF], F32, name=f"g1_{h}")
+            g2 = sb.tile([P, PACK, HALF], F32, name=f"g2_{h}")
+            g3 = sb.tile([P, PACK, HALF], F32, name=f"g3_{h}")
+            pa = sb.tile([P, PACK, HALF], F32, name=f"pa_{h}")
+            pc = sb.tile([P, PACK, HALF], F32, name=f"pc_{h}")
+            for t in range(PACK):
+                gather("s" if (h == 0 and t < 2) else "v", g1[:, t, :], y_win[t], n1_t, h)
+                gather("s", g2[:, t, :], y_win[t], n2_t, h)
+                gather("s", g3[:, t, :], y_win[t], n3_t, h)
+                nc.vector.scalar_tensor_tensor(pa[:, t, :], g1[:, t, :], coef[:, t : t + 1], y_ps[h][t // 2][:, t % 2, :], ALU.mult, ALU.mult)
+                nc.vector.scalar_tensor_tensor(pc[:, t, :], g2[:, t, :], coef[:, t : t + 1], g3[:, t, :], ALU.mult, ALU.mult)
+            z_bf = sb.tile([P, HALF * PACK], BF16, name=f"z_bf{h}", align_bytes=64)
+            nc.vector.tensor_tensor(
+                z_bf[:].rearrange("p (c i t) -> p c t i", t=PACK, i=2),
+                pa[:].rearrange("p t (c i) -> p c t i", i=2),
+                pc[:].rearrange("p t (c i) -> p c t i", i=2),
+                ALU.add,
+            )
+            z_codes = sb.tile([P, HALF], U32, name=f"z_codes{h}", align_bytes=64)
+            z_scales = sb.tile([P, HALF], U8, name=f"z_scales{h}", align_bytes=64)
+            nc.vector.quantize_mx(out=z_codes[:].bitcast(FP8X4), scales=z_scales[:], in_=z_bf[:])
+            for t in range(PACK):
+                nc.tensor.matmul_mx(
+                    out=h_ps[h][t // 2][:, t % 2, :],
+                    lhsT=dw_dealt[:, P * t : P * (t + 1)].bitcast(FP8X4),
+                    lhsT_scale=ds_dealt[:, P * t : P * (t + 1)],
+                    rhs=z_codes[:].bitcast(FP8X4),
+                    rhs_scale=z_scales[:],
+                    start=True,
+                    stop=True,
+                )
+            for t in range(PACK):
+                nc.scalar.activation(th_win[t][:, HALF * h : HALF * (h + 1)], h_ps[h][t // 2][:, t % 2, :], ACT.Tanh, scale=0.03125)
+
+        out_rows = out.rearrange("(p t) n -> p t n", t=PACK)
+        st_win = [sb.tile([P, S], F32, name=f"st_win{t}") for t in range(PACK)]
+        g4 = [sb.tile([P, S], F32, name=f"g4_{t}") for t in range(PACK)]
+        g5 = [sb.tile([P, S], F32, name=f"g5_{t}") for t in range(PACK)]
+        res = [sb.tile([P, S], F32, name=f"res{t}") for t in range(PACK)]
+
+        def gate(t):
+            for h in range(2):
+                cols = slice(HALF * h, HALF * (h + 1))
+                gather("s", g4[t][:, cols], th_win[t], n4_t, h, 0.03125, 0.03125)
+                nc.vector.tensor_tensor(st_win[t][:, cols], g4[t][:, cols], h_ps[h][t // 2][:, t % 2, :], ALU.mult)
+
+        def finish(t):
+            for h in range(2):
+                cols = slice(HALF * h, HALF * (h + 1))
+                gather("v" if h == 0 else "s", g5[t][:, cols], st_win[t], n5_t, h)
+            nc.vector.tensor_tensor(res[t][:], st_win[t][:], g5[t][:], ALU.subtract)
+            nc.sync.dma_start(out_rows[:, t, :], res[t][:])
+
+        gate(0)
+        for t in range(PACK):
+            if t + 1 < PACK:
+                gate(t + 1)
+            finish(t)

@@ -49,46 +49,35 @@ def tile_picked_densedothopg_none_p_kernel(tc, x_words, x_scales, w1, gs, d_word
         ds_win = sb.tile([P, G], U8, name="ds_win")
         nc.gpsimd.memset(xs_win[:].bitcast(I32), 0)
         nc.vector.memset(ds_win[:].bitcast(I32), 0)
-        offs_t = load_list(offs, "offs_t")
-        k1_t = load_list(k1, "k1_t")
         w_rows = w1.rearrange("(p j) c -> p j c", j=PACK)
-        w_raw = [sb.tile([P, PACK, H // 2], F32, name=f"w_raw{a}") for a in range(2)]
-        nc.sync.dma_start(w_raw[0][:], w_rows[:, :, 0 : H // 2])
+        w_raw = [sb.tile([P, PACK, H // 2], F32, name=f"w_raw{a}", tag=f"big{a}") for a in range(2)]
+        offs_t = load_list(offs, "offs_t")
         for q in range(4):
-            nc.gpsimd.dma_start(xs_win[32 * q : 32 * q + 4, :].bitcast(I32), x_scales[0][4 * q : 4 * q + 4, :].bitcast(I32))
-        n1_t = load_list(n1, "n1_t")
-        n2_t = load_list(n2, "n2_t")
+            nc.scalar.dma_start(xs_win[32 * q : 32 * q + 4, :].bitcast(I32), x_scales[0][4 * q : 4 * q + 4, :].bitcast(I32))
+        nc.sync.dma_start(w_raw[0][:], w_rows[:, :, 0 : H // 2])
         nc.sync.dma_start(w_raw[1][:], w_rows[:, :, H // 2 : H])
-        xw_win = sb.tile([P, T], I32, name="xw_win")
+        xw_win = sb.tile([P, T], I32, name="xw_win", tag="xw", align_bytes=64)
         nc.sync.dma_start(xw_win[:], x_words[0].rearrange("p n t -> p (n t)").bitcast(I32))
+        k1_t = load_list(k1, "k1_t")
         for r in range(2):
-            nc.scalar.dma_start(ds_win[r:P:16, :].bitcast(I32), d_scales[0][r:16:2, :].bitcast(I32))
-        gs_t = sb.tile([P, PACK], F32, name="gs_t")
-        nc.gpsimd.dma_start(gs_t[:], gs.rearrange("(p t) o -> p (t o)", t=PACK))
+            nc.sync.dma_start(ds_win[r:P:16, :].bitcast(I32), d_scales[0][r:16:2, :].bitcast(I32))
+        n2_t = load_list(n2, "n2_t")
+        n1_t = load_list(n1, "n1_t")
         n3_t = load_list(n3, "n3_t")
         dw_win = sb.tile([P, G], I32, name="dw_win")
         nc.sync.dma_start(dw_win[:], d_words[0].rearrange("p n t -> p (n t)").bitcast(I32))
         n4_t = load_list(n4, "n4_t")
         n5_t = load_list(n5, "n5_t")
+        gs_t = sb.tile([P, PACK], F32, name="gs_t")
+        nc.gpsimd.dma_start(gs_t[:], gs.rearrange("(p t) o -> p (t o)", t=PACK))
         coef = sb.tile([P, PACK], F32, name="coef")
         nc.gpsimd.tensor_scalar(coef[:], gs_t[:], 0.75, 0.0, ALU.mult, ALU.add)
 
-        xs_g = sb.tile([P, S], U8, name="xs_g", align_bytes=64)
-        nc.vector.tensor_copy(xs_g[:], xs_win[:].indirect(offs_t[:]))
-        ds_g = sb.tile([P, H], U8, name="ds_g", align_bytes=64)
-        nc.vector.tensor_copy(ds_g[:], ds_win[:].indirect(k1_t[:]))
-        ds_dealt = sb.tile([P, H], U8, name="ds_dealt", align_bytes=64)
-        nc.vector.tensor_copy(
-            ds_dealt[:].rearrange("p (t c i) -> p c t i", t=PACK, i=16),
-            ds_g[:].rearrange("p (c i t) -> p c t i", t=PACK, i=16),
-        )
-        for r in range(2):
-            nc.sync.dma_start(ds_dealt[2 + r : P : 32, :].bitcast(I32), ds_dealt[16 + r : P : 32, :].bitcast(I32))
 
         w_bf = sb.tile([P, PACK * H], BF16, name="w_bf", align_bytes=64)
         w_view = w_bf[:].rearrange("p (t m j) -> p m t j", t=PACK, j=PACK)
         for a in range(2):
-            nc.scalar.activation(w_view[:, 64 * a : 64 * (a + 1)], w_raw[a][:].rearrange("p j (m t) -> p m t j", t=PACK), ACT.Copy)
+            nc.scalar.copy(w_view[:, 64 * a : 64 * (a + 1)], w_raw[a][:].rearrange("p j (m t) -> p m t j", t=PACK))
         w_codes = sb.tile([P, H], U32, name="w_codes", align_bytes=64)
         w_scales = sb.tile([P, H], U8, name="w_scales", align_bytes=64)
         nc.vector.quantize_mx(out=w_codes[:].bitcast(FP8X4), scales=w_scales[:], in_=w_bf[:])
@@ -96,6 +85,8 @@ def tile_picked_densedothopg_none_p_kernel(tc, x_words, x_scales, w1, gs, d_word
         y_ps = [[psum.tile([P, 2, HALF], F32, name=f"y_ps{h}{u}") for u in range(2)] for h in range(2)]
         y_win = [sb.tile([P, S], F32, name=f"y_win{t}") for t in range(PACK)]
         for h in range(2):
+            xs_g = sb.tile([P, HALF], U8, name=f"xs_g{h}", align_bytes=64)
+            nc.vector.tensor_copy(xs_g[:], xs_win[:].indirect(offs_t[:, 16 * h : 16 * (h + 1)]))
             xw_g = sb.tile([P, HALF], U32, name=f"xw_g{h}", align_bytes=64)
             nc.vector.tensor_copy(xw_g[:], xw_win[:].bitcast(U32).indirect(offs_t[:, 16 * h : 16 * (h + 1)]))
             for t in range(PACK):
@@ -104,13 +95,25 @@ def tile_picked_densedothopg_none_p_kernel(tc, x_words, x_scales, w1, gs, d_word
                     lhsT=w_codes[:, P * t : P * (t + 1)].bitcast(FP8X4),
                     lhsT_scale=w_scales[:, P * t : P * (t + 1)],
                     rhs=xw_g[:].bitcast(FP8X4),
-                    rhs_scale=xs_g[:, HALF * h : HALF * (h + 1)],
+                    rhs_scale=xs_g[:],
                     start=True,
                     stop=True,
                 )
             for t in range(PACK):
-                nc.scalar.activation(y_win[t][:, HALF * h : HALF * (h + 1)], y_ps[h][t // 2][:, t % 2, :], ACT.Copy)
+                if False:
+                    nc.vector.tensor_copy(y_win[t][:, HALF * h : HALF * (h + 1)], y_ps[h][t // 2][:, t % 2, :])
+                else:
+                    nc.scalar.activation(y_win[t][:, HALF * h : HALF * (h + 1)], y_ps[h][t // 2][:, t % 2, :], ACT.Copy)
 
+        ds_g = sb.tile([P, H], U8, name="ds_g", tag="xw", align_bytes=64)
+        nc.vector.tensor_copy(ds_g[:], ds_win[:].indirect(k1_t[:]))
+        ds_dealt = sb.tile([P, H], U8, name="ds_dealt", align_bytes=64)
+        nc.vector.tensor_copy(
+            ds_dealt[:].rearrange("p (t c i) -> p c t i", t=PACK, i=16),
+            ds_g[:].rearrange("p (c i t) -> p c t i", t=PACK, i=16),
+        )
+        for r in range(2):
+            nc.sync.dma_start(ds_dealt[2 + r : P : 32, :].bitcast(I32), ds_dealt[16 + r : P : 32, :].bitcast(I32))
         dw_g = sb.tile([P, H], U32, name="dw_g", align_bytes=64)
         nc.vector.tensor_copy(dw_g[:], dw_win[:].bitcast(U32).indirect(k1_t[:]))
         dw_dealt = sb.tile([P, H], U32, name="dw_dealt", align_bytes=64)
@@ -121,24 +124,33 @@ def tile_picked_densedothopg_none_p_kernel(tc, x_words, x_scales, w1, gs, d_word
 
         h_ps = [[psum.tile([P, 2, HALF], F32, name=f"h_ps{h}{u}") for u in range(2)] for h in range(2)]
         th_win = [sb.tile([P, S], F32, name=f"th_win{t}") for t in range(PACK)]
+        def tanh_out(h):
+            for t in range(PACK):
+                nc.scalar.activation(th_win[t][:, HALF * h : HALF * (h + 1)], h_ps[h][t // 2][:, t % 2, :], ACT.Tanh, scale=0.03125)
+
         for h in range(2):
             g1 = sb.tile([P, PACK, HALF], F32, name=f"g1_{h}")
             g2 = sb.tile([P, PACK, HALF], F32, name=f"g2_{h}")
             g3 = sb.tile([P, PACK, HALF], F32, name=f"g3_{h}")
             pa = sb.tile([P, PACK, HALF], F32, name=f"pa_{h}")
-            pc = sb.tile([P, PACK, HALF], F32, name=f"pc_{h}")
+            pc = sb.tile([P, PACK, HALF], F32, name=f"pc_{h}", tag=f"pc_{h}", align_bytes=64)
+            z_pl = sb.tile([P, PACK, HALF], BF16, name=f"z_pl{h}")
             for t in range(PACK):
-                gather("s" if (h == 0 and t < 2) else "v", g1[:, t, :], y_win[t], n1_t, h)
                 gather("s", g2[:, t, :], y_win[t], n2_t, h)
-                gather("s", g3[:, t, :], y_win[t], n3_t, h)
+                gather("s" if (True) else "v", g1[:, t, :], y_win[t], n1_t, h)
+                if True:
+                    nc.vector.tensor_tensor(pc[:, t, :], y_win[t][:].indirect(n3_t[:, 16 * h : 16 * (h + 1)]), g2[:, t, :], ALU.mult)
+                else:
+                    gather("s", g3[:, t, :], y_win[t], n3_t, h)
+                    nc.vector.tensor_tensor(pc[:, t, :], g3[:, t, :], g2[:, t, :], ALU.mult)
                 nc.vector.scalar_tensor_tensor(pa[:, t, :], g1[:, t, :], coef[:, t : t + 1], y_ps[h][t // 2][:, t % 2, :], ALU.mult, ALU.mult)
-                nc.vector.scalar_tensor_tensor(pc[:, t, :], g2[:, t, :], coef[:, t : t + 1], g3[:, t, :], ALU.mult, ALU.mult)
+                if t > 0:
+                    nc.vector.scalar_tensor_tensor(z_pl[:, t - 1, :], pc[:, t - 1, :], coef[:, t - 1 : t], pa[:, t - 1, :], ALU.mult, ALU.add)
+            nc.vector.scalar_tensor_tensor(z_pl[:, 3, :], pc[:, 3, :], coef[:, 3:4], pa[:, 3, :], ALU.mult, ALU.add)
             z_bf = sb.tile([P, HALF * PACK], BF16, name=f"z_bf{h}", align_bytes=64)
-            nc.vector.tensor_tensor(
-                z_bf[:].rearrange("p (c i t) -> p c t i", t=PACK, i=2),
-                pa[:].rearrange("p t (c i) -> p c t i", i=2),
-                pc[:].rearrange("p t (c i) -> p c t i", i=2),
-                ALU.add,
+            nc.vector.tensor_copy(
+                z_bf[:].rearrange("p (c i t) -> p c t i", t=PACK, i=4),
+                z_pl[:].rearrange("p t (c i) -> p c t i", i=4),
             )
             z_codes = sb.tile([P, HALF], U32, name=f"z_codes{h}", align_bytes=64)
             z_scales = sb.tile([P, HALF], U8, name=f"z_scales{h}", align_bytes=64)
@@ -153,8 +165,8 @@ def tile_picked_densedothopg_none_p_kernel(tc, x_words, x_scales, w1, gs, d_word
                     start=True,
                     stop=True,
                 )
-            for t in range(PACK):
-                nc.scalar.activation(th_win[t][:, HALF * h : HALF * (h + 1)], h_ps[h][t // 2][:, t % 2, :], ACT.Tanh, scale=0.03125)
+        tanh_out(0)
+        tanh_out(1)
 
         out_rows = out.rearrange("(p t) n -> p t n", t=PACK)
         st_win = [sb.tile([P, S], F32, name=f"st_win{t}") for t in range(PACK)]
@@ -165,15 +177,17 @@ def tile_picked_densedothopg_none_p_kernel(tc, x_words, x_scales, w1, gs, d_word
         def gate(t):
             for h in range(2):
                 cols = slice(HALF * h, HALF * (h + 1))
-                gather("s", g4[t][:, cols], th_win[t], n4_t, h, 0.03125, 0.03125)
+                gather("v" if (t == 0 and h == 1) else "s", g4[t][:, cols], th_win[t], n4_t, h, 0.03125, 0.03125)
                 nc.vector.tensor_tensor(st_win[t][:, cols], g4[t][:, cols], h_ps[h][t // 2][:, t % 2, :], ALU.mult)
 
         def finish(t):
             for h in range(2):
                 cols = slice(HALF * h, HALF * (h + 1))
-                gather("v" if h == 0 else "s", g5[t][:, cols], st_win[t], n5_t, h)
-            nc.vector.tensor_tensor(res[t][:], st_win[t][:], g5[t][:], ALU.subtract)
-            nc.sync.dma_start(out_rows[:, t, :], res[t][:])
+                gather("s" if (h == 1) else "v", g5[t][:, cols], st_win[t], n5_t, h)
+            pieces = [slice(0, S)] if t + 1 < PACK else [slice(0, HALF), slice(HALF, S)]
+            for cols in pieces:
+                nc.vector.tensor_tensor(res[t][:, cols], st_win[t][:, cols], g5[t][:, cols], ALU.subtract)
+                nc.sync.dma_start(out_rows[:, t, cols], res[t][:, cols])
 
         gate(0)
         for t in range(PACK):

@@ -18,6 +18,8 @@ ALU = mybir.AluOpType
 P = 128
 PACK = 4
 HALF = S // 2
+HALVES = [slice(0, HALF), slice(HALF, S)]
+ALL = slice(0, S)
 
 
 def tile_picked_densedothopg_none_p_kernel(tc, x_words, x_scales, w1, gs, d_words, d_scales, offs, n1, n2, n3, k1, n4, n5, out):
@@ -32,29 +34,22 @@ def tile_picked_densedothopg_none_p_kernel(tc, x_words, x_scales, w1, gs, d_word
             nc.sync.dma_start(tile[:], src)
             return tile
 
-        def gather(eng, dst, window, lst, h, scale=None, bias=None):
-            src = window[:].indirect(lst[:, h * (HALF // 16) : (h + 1) * (HALF // 16)])
-            if eng == "v":
-                if scale is None:
-                    nc.vector.tensor_copy(dst, src)
-                else:
-                    nc.vector.tensor_scalar(dst, src, scale, bias, ALU.mult, ALU.add)
-            else:
-                if scale is None:
-                    nc.scalar.activation(dst, src, ACT.Copy)
-                else:
-                    nc.scalar.activation(dst, src, ACT.Copy, bias=bias, scale=scale)
+        def picked(window, lst, cols):
+            return window.indirect(lst[:, cols.start // 16 : cols.stop // 16])
 
         xs_win = sb.tile([P, T], U8, name="xs_win")
         ds_win = sb.tile([P, G], U8, name="ds_win")
         nc.gpsimd.memset(xs_win[:].bitcast(I32), 0)
         nc.vector.memset(ds_win[:].bitcast(I32), 0)
+        rows = [sb.tile([P, 2 * S], F32, name=f"rows{t}") for t in range(PACK)]
+        for t in range(PACK):
+            nc.vector.memset(rows[t][:, S : 2 * S], 0.0)
         w_rows = w1.rearrange("(p j) c -> p j c", j=PACK)
-        w_raw = [sb.tile([P, PACK, H // 2], F32, name=f"w_raw{a}", tag=f"big{a}") for a in range(2)]
+        w_raw = [sb.tile([P, PACK, H // 2], F32, name=f"w_raw{a}") for a in range(2)]
         offs_t = load_list(offs, "offs_t")
-        for q in range(4):
-            nc.scalar.dma_start(xs_win[32 * q : 32 * q + 4, :].bitcast(I32), x_scales[0][4 * q : 4 * q + 4, :].bitcast(I32))
         nc.sync.dma_start(w_raw[0][:], w_rows[:, :, 0 : H // 2])
+        for q in range(4):
+            nc.sync.dma_start(xs_win[32 * q : 32 * q + 4, :].bitcast(I32), x_scales[0][4 * q : 4 * q + 4, :].bitcast(I32))
         nc.sync.dma_start(w_raw[1][:], w_rows[:, :, H // 2 : H])
         xw_win = sb.tile([P, T], I32, name="xw_win", tag="xw", align_bytes=64)
         nc.sync.dma_start(xw_win[:], x_words[0].rearrange("p n t -> p (n t)").bitcast(I32))
@@ -64,7 +59,7 @@ def tile_picked_densedothopg_none_p_kernel(tc, x_words, x_scales, w1, gs, d_word
         n2_t = load_list(n2, "n2_t")
         n1_t = load_list(n1, "n1_t")
         n3_t = load_list(n3, "n3_t")
-        dw_win = sb.tile([P, G], I32, name="dw_win")
+        dw_win = sb.tile([P, G], I32, name="dw_win", tag="dw", align_bytes=64)
         nc.sync.dma_start(dw_win[:], d_words[0].rearrange("p n t -> p (n t)").bitcast(I32))
         n4_t = load_list(n4, "n4_t")
         n5_t = load_list(n5, "n5_t")
@@ -73,40 +68,41 @@ def tile_picked_densedothopg_none_p_kernel(tc, x_words, x_scales, w1, gs, d_word
         coef = sb.tile([P, PACK], F32, name="coef")
         nc.gpsimd.tensor_scalar(coef[:], gs_t[:], 0.75, 0.0, ALU.mult, ALU.add)
 
-
         w_bf = sb.tile([P, PACK * H], BF16, name="w_bf", align_bytes=64)
         w_view = w_bf[:].rearrange("p (t m j) -> p m t j", t=PACK, j=PACK)
-        for a in range(2):
-            nc.scalar.copy(w_view[:, 64 * a : 64 * (a + 1)], w_raw[a][:].rearrange("p j (m t) -> p m t j", t=PACK))
+        w_in = [w_raw[a][:].rearrange("p j (m t) -> p m t j", t=PACK) for a in range(2)]
+        nc.scalar.copy(w_view[:, 0:64], w_in[0])
+        nc.scalar.copy(w_view[:, 64:96], w_in[1][:, 0 : 96 - 64])
+        nc.vector.tensor_copy(w_view[:, 96:128], w_in[1][:, 96 - 64 : 64])
         w_codes = sb.tile([P, H], U32, name="w_codes", align_bytes=64)
         w_scales = sb.tile([P, H], U8, name="w_scales", align_bytes=64)
         nc.vector.quantize_mx(out=w_codes[:].bitcast(FP8X4), scales=w_scales[:], in_=w_bf[:])
 
+        xs_g = sb.tile([P, S], U8, name="xs_g", align_bytes=64)
+        nc.vector.tensor_copy(xs_g[:], picked(xs_win[:], offs_t, ALL))
         y_ps = [[psum.tile([P, 2, HALF], F32, name=f"y_ps{h}{u}") for u in range(2)] for h in range(2)]
-        y_win = [sb.tile([P, S], F32, name=f"y_win{t}") for t in range(PACK)]
-        for h in range(2):
-            xs_g = sb.tile([P, HALF], U8, name=f"xs_g{h}", align_bytes=64)
-            nc.vector.tensor_copy(xs_g[:], xs_win[:].indirect(offs_t[:, 16 * h : 16 * (h + 1)]))
+        for h, cols in enumerate(HALVES):
             xw_g = sb.tile([P, HALF], U32, name=f"xw_g{h}", align_bytes=64)
-            nc.vector.tensor_copy(xw_g[:], xw_win[:].bitcast(U32).indirect(offs_t[:, 16 * h : 16 * (h + 1)]))
+            nc.vector.tensor_copy(xw_g[:], picked(xw_win[:].bitcast(U32), offs_t, cols))
             for t in range(PACK):
                 nc.tensor.matmul_mx(
                     out=y_ps[h][t // 2][:, t % 2, :],
                     lhsT=w_codes[:, P * t : P * (t + 1)].bitcast(FP8X4),
                     lhsT_scale=w_scales[:, P * t : P * (t + 1)],
                     rhs=xw_g[:].bitcast(FP8X4),
-                    rhs_scale=xs_g[:],
+                    rhs_scale=xs_g[:, cols],
                     start=True,
                     stop=True,
                 )
-            for t in range(PACK):
-                if False:
-                    nc.vector.tensor_copy(y_win[t][:, HALF * h : HALF * (h + 1)], y_ps[h][t // 2][:, t % 2, :])
-                else:
-                    nc.scalar.activation(y_win[t][:, HALF * h : HALF * (h + 1)], y_ps[h][t // 2][:, t % 2, :], ACT.Copy)
+
+        def y_out(h, t):
+            nc.scalar.activation(rows[t][:, HALVES[h]], y_ps[h][t // 2][:, t % 2, :], ACT.Copy)
+
+        for t in range(PACK):
+            y_out(0, t)
 
         ds_g = sb.tile([P, H], U8, name="ds_g", tag="xw", align_bytes=64)
-        nc.vector.tensor_copy(ds_g[:], ds_win[:].indirect(k1_t[:]))
+        nc.vector.tensor_copy(ds_g[:], picked(ds_win[:], k1_t, ALL))
         ds_dealt = sb.tile([P, H], U8, name="ds_dealt", align_bytes=64)
         nc.vector.tensor_copy(
             ds_dealt[:].rearrange("p (t c i) -> p c t i", t=PACK, i=16),
@@ -114,83 +110,85 @@ def tile_picked_densedothopg_none_p_kernel(tc, x_words, x_scales, w1, gs, d_word
         )
         for r in range(2):
             nc.sync.dma_start(ds_dealt[2 + r : P : 32, :].bitcast(I32), ds_dealt[16 + r : P : 32, :].bitcast(I32))
-        dw_g = sb.tile([P, H], U32, name="dw_g", align_bytes=64)
-        nc.vector.tensor_copy(dw_g[:], dw_win[:].bitcast(U32).indirect(k1_t[:]))
+        dw_g = sb.tile([P, H], U32, name="dw_g", tag="dg", align_bytes=64)
+        nc.vector.tensor_copy(dw_g[:], picked(dw_win[:].bitcast(U32), k1_t, ALL))
         dw_dealt = sb.tile([P, H], U32, name="dw_dealt", align_bytes=64)
         nc.vector.tensor_copy(
             dw_dealt[:].rearrange("p (t c i) -> p c t i", t=PACK, i=4),
             dw_g[:].rearrange("p (c i t) -> p c t i", t=PACK, i=4),
         )
 
-        h_ps = [[psum.tile([P, 2, HALF], F32, name=f"h_ps{h}{u}") for u in range(2)] for h in range(2)]
-        th_win = [sb.tile([P, S], F32, name=f"th_win{t}") for t in range(PACK)]
-        def tanh_out(h):
-            for t in range(PACK):
-                nc.scalar.activation(th_win[t][:, HALF * h : HALF * (h + 1)], h_ps[h][t // 2][:, t % 2, :], ACT.Tanh, scale=0.03125)
+        pa = sb.tile([P, PACK, S], F32, name="pa", tag="dw", align_bytes=64)
+        pc = sb.tile([P, PACK, S], F32, name="pc", tag="dg", align_bytes=64)
+        z_pl = sb.tile([P, PACK, S], BF16, name="z_pl")
+        for t in range(PACK):
+            y_out(1, t)
+            g2 = sb.tile([P, S], F32, name=f"g2_{t}")
+            g1 = sb.tile([P, S], F32, name=f"g1_{t}")
+            nc.scalar.activation(g2[:], picked(rows[t][:], n2_t, ALL), ACT.Copy)
+            nc.scalar.activation(g1[:], picked(rows[t][:], n1_t, ALL), ACT.Copy)
+            if False:
+                g3 = sb.tile([P, S], F32, name=f"g3_{t}")
+                nc.scalar.activation(g3[:], picked(rows[t][:], n3_t, ALL), ACT.Copy)
+                nc.vector.tensor_tensor(pc[:, t, :], g3[:], g2[:], ALU.mult)
+            else:
+                nc.vector.tensor_tensor(pc[:, t, :], picked(rows[t][:], n3_t, ALL), g2[:], ALU.mult)
+            nc.vector.scalar_tensor_tensor(pa[:, t, :], g1[:], coef[:, t : t + 1], rows[t][:, ALL], ALU.mult, ALU.mult)
+            nc.vector.scalar_tensor_tensor(z_pl[:, t, :], pc[:, t, :], coef[:, t : t + 1], pa[:, t, :], ALU.mult, ALU.add)
 
-        for h in range(2):
-            g1 = sb.tile([P, PACK, HALF], F32, name=f"g1_{h}")
-            g2 = sb.tile([P, PACK, HALF], F32, name=f"g2_{h}")
-            g3 = sb.tile([P, PACK, HALF], F32, name=f"g3_{h}")
-            pa = sb.tile([P, PACK, HALF], F32, name=f"pa_{h}")
-            pc = sb.tile([P, PACK, HALF], F32, name=f"pc_{h}", tag=f"pc_{h}", align_bytes=64)
-            z_pl = sb.tile([P, PACK, HALF], BF16, name=f"z_pl{h}")
-            for t in range(PACK):
-                gather("s", g2[:, t, :], y_win[t], n2_t, h)
-                gather("s" if (True) else "v", g1[:, t, :], y_win[t], n1_t, h)
-                if True:
-                    nc.vector.tensor_tensor(pc[:, t, :], y_win[t][:].indirect(n3_t[:, 16 * h : 16 * (h + 1)]), g2[:, t, :], ALU.mult)
-                else:
-                    gather("s", g3[:, t, :], y_win[t], n3_t, h)
-                    nc.vector.tensor_tensor(pc[:, t, :], g3[:, t, :], g2[:, t, :], ALU.mult)
-                nc.vector.scalar_tensor_tensor(pa[:, t, :], g1[:, t, :], coef[:, t : t + 1], y_ps[h][t // 2][:, t % 2, :], ALU.mult, ALU.mult)
-                if t > 0:
-                    nc.vector.scalar_tensor_tensor(z_pl[:, t - 1, :], pc[:, t - 1, :], coef[:, t - 1 : t], pa[:, t - 1, :], ALU.mult, ALU.add)
-            nc.vector.scalar_tensor_tensor(z_pl[:, 3, :], pc[:, 3, :], coef[:, 3:4], pa[:, 3, :], ALU.mult, ALU.add)
-            z_bf = sb.tile([P, HALF * PACK], BF16, name=f"z_bf{h}", align_bytes=64)
-            nc.vector.tensor_copy(
-                z_bf[:].rearrange("p (c i t) -> p c t i", t=PACK, i=4),
-                z_pl[:].rearrange("p t (c i) -> p c t i", i=4),
+        h_ps = [psum.tile([P, S], F32, name=f"h_ps{t}") for t in range(PACK)]
+        z_bf = sb.tile([P, S * PACK], BF16, name="z_bf", align_bytes=64)
+        z_to = z_bf[:].rearrange("p (c i t) -> p c t i", t=PACK, i=4)
+        z_from = z_pl[:].rearrange("p t (c i) -> p c t i", i=4)
+        nc.vector.tensor_copy(z_to[:, 0:96], z_from[:, 0:96])
+        nc.scalar.copy(z_to[:, 96:128], z_from[:, 96:128])
+        z_codes = sb.tile([P, S], U32, name="z_codes", align_bytes=64)
+        z_scales = sb.tile([P, S], U8, name="z_scales", align_bytes=64)
+        nc.vector.quantize_mx(out=z_codes[:].bitcast(FP8X4), scales=z_scales[:], in_=z_bf[:])
+        for t in range(PACK):
+            nc.tensor.matmul_mx(
+                out=h_ps[t][:],
+                lhsT=dw_dealt[:, P * t : P * (t + 1)].bitcast(FP8X4),
+                lhsT_scale=ds_dealt[:, P * t : P * (t + 1)],
+                rhs=z_codes[:].bitcast(FP8X4),
+                rhs_scale=z_scales[:],
+                start=True,
+                stop=True,
             )
-            z_codes = sb.tile([P, HALF], U32, name=f"z_codes{h}", align_bytes=64)
-            z_scales = sb.tile([P, HALF], U8, name=f"z_scales{h}", align_bytes=64)
-            nc.vector.quantize_mx(out=z_codes[:].bitcast(FP8X4), scales=z_scales[:], in_=z_bf[:])
-            for t in range(PACK):
-                nc.tensor.matmul_mx(
-                    out=h_ps[h][t // 2][:, t % 2, :],
-                    lhsT=dw_dealt[:, P * t : P * (t + 1)].bitcast(FP8X4),
-                    lhsT_scale=ds_dealt[:, P * t : P * (t + 1)],
-                    rhs=z_codes[:].bitcast(FP8X4),
-                    rhs_scale=z_scales[:],
-                    start=True,
-                    stop=True,
-                )
-        tanh_out(0)
-        tanh_out(1)
 
         out_rows = out.rearrange("(p t) n -> p t n", t=PACK)
-        st_win = [sb.tile([P, S], F32, name=f"st_win{t}") for t in range(PACK)]
-        g4 = [sb.tile([P, S], F32, name=f"g4_{t}") for t in range(PACK)]
-        g5 = [sb.tile([P, S], F32, name=f"g5_{t}") for t in range(PACK)]
-        res = [sb.tile([P, S], F32, name=f"res{t}") for t in range(PACK)]
 
-        def gate(t):
-            for h in range(2):
-                cols = slice(HALF * h, HALF * (h + 1))
-                gather("v" if (t == 0 and h == 1) else "s", g4[t][:, cols], th_win[t], n4_t, h, 0.03125, 0.03125)
-                nc.vector.tensor_tensor(st_win[t][:, cols], g4[t][:, cols], h_ps[h][t // 2][:, t % 2, :], ALU.mult)
+        def tanh_out(t):
+            nc.scalar.activation(rows[t][:, ALL], h_ps[t][:], ACT.Tanh, scale=0.03125)
 
-        def finish(t):
-            for h in range(2):
-                cols = slice(HALF * h, HALF * (h + 1))
-                gather("s" if (h == 1) else "v", g5[t][:, cols], st_win[t], n5_t, h)
-            pieces = [slice(0, S)] if t + 1 < PACK else [slice(0, HALF), slice(HALF, S)]
+        def gate(t, on_scalar, on_vector):
+            g4 = sb.tile([P, S], F32, name=f"g4_{t}")
+            for cols in on_scalar:
+                nc.scalar.activation(g4[:, cols], picked(rows[t][:], n4_t, cols), ACT.Copy, bias=0.03125, scale=0.03125)
+            for cols in on_vector:
+                nc.vector.tensor_scalar(g4[:, cols], picked(rows[t][:], n4_t, cols), 0.03125, 0.03125, ALU.mult, ALU.add)
+            nc.vector.tensor_tensor(rows[t][:, ALL], g4[:], h_ps[t][:], ALU.mult)
+
+        def finish(t, pieces, on_vector, sub):
+            g5 = sb.tile([P, S], F32, name=f"g5_{t}")
+            res = sb.tile([P, S], F32, name=f"res{t}")
             for cols in pieces:
-                nc.vector.tensor_tensor(res[t][:, cols], st_win[t][:, cols], g5[t][:, cols], ALU.subtract)
-                nc.sync.dma_start(out_rows[:, t, cols], res[t][:, cols])
+                if on_vector(cols):
+                    nc.vector.tensor_copy(g5[:, cols], picked(rows[t][:], n5_t, cols))
+                else:
+                    nc.scalar.activation(g5[:, cols], picked(rows[t][:], n5_t, cols), ACT.Copy)
+            for cols in pieces:
+                sub.tensor_tensor(res[:, cols], rows[t][:, cols], g5[:, cols], ALU.subtract)
+                nc.sync.dma_start(out_rows[:, t, cols], res[:, cols])
 
-        gate(0)
-        for t in range(PACK):
-            if t + 1 < PACK:
-                gate(t + 1)
-            finish(t)
+        tanh_out(0)
+        gate(0, [HALVES[0]], [HALVES[1]])
+        for t in range(1, PACK):
+            tanh_out(t)
+        gate(1, [], [ALL])
+        gate(2, [ALL], [])
+        gate(3, [ALL], [])
+        finish(0, [ALL], lambda c: True, nc.vector)
+        finish(1, [ALL], lambda c: False, nc.vector)
+        finish(2, [ALL], lambda c: False, nc.vector)
+        finish(3, HALVES, lambda c: False, nc.vector)

@@ -110,31 +110,32 @@ def tile_picked_densedothopg_none_p_kernel(tc, x_words, x_scales, w1, gs, d_word
         )
         for r in range(2):
             nc.sync.dma_start(ds_dealt[2 + r : P : 32, :].bitcast(I32), ds_dealt[16 + r : P : 32, :].bitcast(I32))
-        dw_g = sb.tile([P, H], U32, name="dw_g", tag="dg", align_bytes=64)
+        dw_g = sb.tile([P, H], U32, name="dw_g", align_bytes=64)
         nc.vector.tensor_copy(dw_g[:], picked(dw_win[:].bitcast(U32), k1_t, ALL))
-        dw_dealt = sb.tile([P, H], U32, name="dw_dealt", align_bytes=64)
-        nc.vector.tensor_copy(
-            dw_dealt[:].rearrange("p (t c i) -> p c t i", t=PACK, i=4),
-            dw_g[:].rearrange("p (c i t) -> p c t i", t=PACK, i=4),
-        )
 
-        pa = sb.tile([P, PACK, S], F32, name="pa", tag="dw", align_bytes=64)
-        pc = sb.tile([P, PACK, S], F32, name="pc", tag="dg", align_bytes=64)
+        prod = sb.tile([P, 2, PACK, S], F32, name="prod", tag="dw", align_bytes=64)
         z_pl = sb.tile([P, PACK, S], BF16, name="z_pl")
+        dw_dealt = sb.tile([P, H], U32, name="dw_dealt", align_bytes=64)
+
+        def z_tile(t):
+            nc.vector.scalar_tensor_tensor(z_pl[:, t, :], prod[:, 1, t, :], coef[:, t : t + 1], prod[:, 0, t, :], ALU.mult, ALU.add)
+
         for t in range(PACK):
             y_out(1, t)
             g2 = sb.tile([P, S], F32, name=f"g2_{t}")
             g1 = sb.tile([P, S], F32, name=f"g1_{t}")
             nc.scalar.activation(g2[:], picked(rows[t][:], n2_t, ALL), ACT.Copy)
             nc.scalar.activation(g1[:], picked(rows[t][:], n1_t, ALL), ACT.Copy)
-            if False:
-                g3 = sb.tile([P, S], F32, name=f"g3_{t}")
-                nc.scalar.activation(g3[:], picked(rows[t][:], n3_t, ALL), ACT.Copy)
-                nc.vector.tensor_tensor(pc[:, t, :], g3[:], g2[:], ALU.mult)
+            nc.vector.tensor_tensor(prod[:, 1, t, :], picked(rows[t][:], n3_t, ALL), g2[:], ALU.mult)
+            if t == 0:
+                nc.vector.tensor_copy(
+                    dw_dealt[:].rearrange("p (t c i) -> p c t i", t=PACK, i=4),
+                    dw_g[:].rearrange("p (c i t) -> p c t i", t=PACK, i=4),
+                )
             else:
-                nc.vector.tensor_tensor(pc[:, t, :], picked(rows[t][:], n3_t, ALL), g2[:], ALU.mult)
-            nc.vector.scalar_tensor_tensor(pa[:, t, :], g1[:], coef[:, t : t + 1], rows[t][:, ALL], ALU.mult, ALU.mult)
-            nc.vector.scalar_tensor_tensor(z_pl[:, t, :], pc[:, t, :], coef[:, t : t + 1], pa[:, t, :], ALU.mult, ALU.add)
+                z_tile(t - 1)
+            nc.vector.scalar_tensor_tensor(prod[:, 0, t, :], g1[:], coef[:, t : t + 1], rows[t][:, ALL], ALU.mult, ALU.mult)
+        z_tile(PACK - 1)
 
         h_ps = [psum.tile([P, S], F32, name=f"h_ps{t}") for t in range(PACK)]
         z_bf = sb.tile([P, S * PACK], BF16, name="z_bf", align_bytes=64)
@@ -161,34 +162,38 @@ def tile_picked_densedothopg_none_p_kernel(tc, x_words, x_scales, w1, gs, d_word
         def tanh_out(t):
             nc.scalar.activation(rows[t][:, ALL], h_ps[t][:], ACT.Tanh, scale=0.03125)
 
-        def gate(t, on_scalar, on_vector):
-            g4 = sb.tile([P, S], F32, name=f"g4_{t}")
-            for cols in on_scalar:
-                nc.scalar.activation(g4[:, cols], picked(rows[t][:], n4_t, cols), ACT.Copy, bias=0.03125, scale=0.03125)
-            for cols in on_vector:
-                nc.vector.tensor_scalar(g4[:, cols], picked(rows[t][:], n4_t, cols), 0.03125, 0.03125, ALU.mult, ALU.add)
-            nc.vector.tensor_tensor(rows[t][:, ALL], g4[:], h_ps[t][:], ALU.mult)
+        g4 = [sb.tile([P, S], F32, name=f"g4_{t}") for t in range(PACK)]
+        g5 = [sb.tile([P, S], F32, name=f"g5_{t}") for t in range(PACK)]
+        res = [sb.tile([P, S], F32, name=f"res{t}") for t in range(PACK)]
 
-        def finish(t, pieces, on_vector, sub):
-            g5 = sb.tile([P, S], F32, name=f"g5_{t}")
-            res = sb.tile([P, S], F32, name=f"res{t}")
-            for cols in pieces:
-                if on_vector(cols):
-                    nc.vector.tensor_copy(g5[:, cols], picked(rows[t][:], n5_t, cols))
-                else:
-                    nc.scalar.activation(g5[:, cols], picked(rows[t][:], n5_t, cols), ACT.Copy)
-            for cols in pieces:
-                sub.tensor_tensor(res[:, cols], rows[t][:, cols], g5[:, cols], ALU.subtract)
-                nc.sync.dma_start(out_rows[:, t, cols], res[:, cols])
+        def gate_on_scalar(t, cols):
+            nc.scalar.activation(g4[t][:, cols], picked(rows[t][:], n4_t, cols), ACT.Copy, bias=0.03125, scale=0.03125)
 
-        tanh_out(0)
-        gate(0, [HALVES[0]], [HALVES[1]])
-        for t in range(1, PACK):
+        def gate_on_vector(t, cols):
+            nc.vector.tensor_scalar(g4[t][:, cols], picked(rows[t][:], n4_t, cols), 0.03125, 0.03125, ALU.mult, ALU.add)
+
+        def st_tile(t):
+            nc.vector.tensor_tensor(rows[t][:, ALL], g4[t][:], h_ps[t][:], ALU.mult)
+
+        def subtract_and_store(engine, t, cols):
+            engine.tensor_tensor(res[t][:, cols], rows[t][:, cols], g5[t][:, cols], ALU.subtract)
+            nc.sync.dma_start(out_rows[:, t, cols], res[t][:, cols])
+
+        for t in (0, 1):
             tanh_out(t)
-        gate(1, [], [ALL])
-        gate(2, [ALL], [])
-        gate(3, [ALL], [])
-        finish(0, [ALL], lambda c: True, nc.vector)
-        finish(1, [ALL], lambda c: False, nc.vector)
-        finish(2, [ALL], lambda c: False, nc.vector)
-        finish(3, HALVES, lambda c: False, nc.vector)
+            gate_on_scalar(t, HALVES[0])
+            gate_on_vector(t, HALVES[1])
+            st_tile(t)
+        for t in (2, 3):
+            tanh_out(t)
+            gate_on_scalar(t, ALL)
+            st_tile(t)
+        for t in (0, 1):
+            nc.vector.tensor_copy(g5[t][:], picked(rows[t][:], n5_t, ALL))
+            subtract_and_store(nc.gpsimd, t, ALL)
+        nc.scalar.activation(g5[2][:], picked(rows[2][:], n5_t, ALL), ACT.Copy)
+        nc.vector.tensor_copy(g5[3][:, HALVES[0]], picked(rows[3][:], n5_t, HALVES[0]))
+        nc.scalar.activation(g5[3][:, HALVES[1]], picked(rows[3][:], n5_t, HALVES[1]), ACT.Copy)
+        subtract_and_store(nc.vector, 2, ALL)
+        for cols in HALVES:
+            subtract_and_store(nc.vector, 3, cols)

from contextlib import ExitStack

import concourse.mybir as mybir

K, T, S, H, G = 512, 2048, 512, 512, 2048
FLOPS = 2 * K * H * S * 2

F32 = mybir.dt.float32
BF16 = mybir.dt.bfloat16
I32 = mybir.dt.int32
U32 = mybir.dt.uint32
U16 = mybir.dt.uint16
U8 = mybir.dt.uint8
FP8X4 = mybir.dt.float8_e4m3fn_x4
ACT = mybir.ActivationFunctionType
ALU = mybir.AluOpType

P = 128
PACK = 4
HALF = S // 2
HALVES = [slice(0, HALF), slice(HALF, S)]
ALL = slice(0, S)


def tile_picked_densedothopg_none_p_kernel(tc, x_words, x_scales, w1, gs, d_words, d_scales, offs, n1, n2, n3, k1, n4, n5, out):
    nc = tc.nc
    with ExitStack() as ctx:
        lists = ctx.enter_context(tc.tile_pool(name="lists", bufs=1))
        sb = ctx.enter_context(tc.tile_pool(name="sb", bufs=1))
        psum = ctx.enter_context(tc.psum_pool(name="psum", bufs=1))

        def load_list(src, name):
            tile = lists.tile([P, S // 16], U16, name=name)
            nc.sync.dma_start(tile[:], src)
            return tile

        def picked(window, lst, cols):
            return window.indirect(lst[:, cols.start // 16 : cols.stop // 16])

        xs_win = sb.tile([P, T], U8, name="xs_win")
        ds_win = sb.tile([P, G], U8, name="ds_win")
        nc.gpsimd.memset(xs_win[:].bitcast(I32), 0)
        nc.vector.memset(ds_win[:].bitcast(I32), 0)
        rows = [sb.tile([P, 2 * S], F32, name=f"rows{t}") for t in range(PACK)]
        for t in range(PACK):
            nc.vector.memset(rows[t][:, S : 2 * S], 0.0)
        w_rows = w1.rearrange("(p j) c -> p j c", j=PACK)
        w_raw = [sb.tile([P, PACK, H // 2], F32, name=f"w_raw{a}") for a in range(2)]
        offs_t = load_list(offs, "offs_t")
        nc.sync.dma_start(w_raw[0][:], w_rows[:, :, 0 : H // 2])
        for q in range(4):
            nc.sync.dma_start(xs_win[32 * q : 32 * q + 4, :].bitcast(I32), x_scales[0][4 * q : 4 * q + 4, :].bitcast(I32))
        nc.sync.dma_start(w_raw[1][:], w_rows[:, :, H // 2 : H])
        xw_win = sb.tile([P, T], I32, name="xw_win", tag="xw", align_bytes=64)
        nc.sync.dma_start(xw_win[:], x_words[0].rearrange("p n t -> p (n t)").bitcast(I32))
        k1_t = load_list(k1, "k1_t")
        for r in range(2):
            nc.sync.dma_start(ds_win[r:P:16, :].bitcast(I32), d_scales[0][r:16:2, :].bitcast(I32))
        n2_t = load_list(n2, "n2_t")
        n1_t = load_list(n1, "n1_t")
        n3_t = load_list(n3, "n3_t")
        dw_win = sb.tile([P, G], I32, name="dw_win", tag="dw", align_bytes=64)
        nc.sync.dma_start(dw_win[:], d_words[0].rearrange("p n t -> p (n t)").bitcast(I32))
        n4_t = load_list(n4, "n4_t")
        n5_t = load_list(n5, "n5_t")
        gs_t = sb.tile([P, PACK], F32, name="gs_t")
        nc.gpsimd.dma_start(gs_t[:], gs.rearrange("(p t) o -> p (t o)", t=PACK))
        coef = sb.tile([P, PACK], F32, name="coef")
        nc.gpsimd.tensor_scalar(coef[:], gs_t[:], 0.75, 0.0, ALU.mult, ALU.add)

        w_bf = sb.tile([P, PACK * H], BF16, name="w_bf", align_bytes=64)
        w_view = w_bf[:].rearrange("p (t m j) -> p m t j", t=PACK, j=PACK)
        w_in = [w_raw[a][:].rearrange("p j (m t) -> p m t j", t=PACK) for a in range(2)]
        nc.scalar.copy(w_view[:, 0:64], w_in[0])
        nc.scalar.copy(w_view[:, 64:96], w_in[1][:, 0 : 96 - 64])
        nc.vector.tensor_copy(w_view[:, 96:128], w_in[1][:, 96 - 64 : 64])
        w_codes = sb.tile([P, H], U32, name="w_codes", align_bytes=64)
        w_scales = sb.tile([P, H], U8, name="w_scales", align_bytes=64)
        nc.vector.quantize_mx(out=w_codes[:].bitcast(FP8X4), scales=w_scales[:], in_=w_bf[:])

        xs_g = sb.tile([P, S], U8, name="xs_g", align_bytes=64)
        nc.vector.tensor_copy(xs_g[:], picked(xs_win[:], offs_t, ALL))
        y_ps = [[psum.tile([P, 2, HALF], F32, name=f"y_ps{h}{u}") for u in range(2)] for h in range(2)]
        for h, cols in enumerate(HALVES):
            xw_g = sb.tile([P, HALF], U32, name=f"xw_g{h}", align_bytes=64)
            nc.vector.tensor_copy(xw_g[:], picked(xw_win[:].bitcast(U32), offs_t, cols))
            for t in range(PACK):
                nc.tensor.matmul_mx(
                    out=y_ps[h][t // 2][:, t % 2, :],
                    lhsT=w_codes[:, P * t : P * (t + 1)].bitcast(FP8X4),
                    lhsT_scale=w_scales[:, P * t : P * (t + 1)],
                    rhs=xw_g[:].bitcast(FP8X4),
                    rhs_scale=xs_g[:, cols],
                    start=True,
                    stop=True,
                )

        def y_out(h, t):
            nc.scalar.activation(rows[t][:, HALVES[h]], y_ps[h][t // 2][:, t % 2, :], ACT.Copy)

        for t in range(PACK):
            y_out(0, t)

        ds_g = sb.tile([P, H], U8, name="ds_g", tag="xw", align_bytes=64)
        nc.vector.tensor_copy(ds_g[:], picked(ds_win[:], k1_t, ALL))
        ds_dealt = sb.tile([P, H], U8, name="ds_dealt", align_bytes=64)
        nc.vector.tensor_copy(
            ds_dealt[:].rearrange("p (t c i) -> p c t i", t=PACK, i=16),
            ds_g[:].rearrange("p (c i t) -> p c t i", t=PACK, i=16),
        )
        for r in range(2):
            nc.sync.dma_start(ds_dealt[2 + r : P : 32, :].bitcast(I32), ds_dealt[16 + r : P : 32, :].bitcast(I32))
        dw_g = sb.tile([P, H], U32, name="dw_g", align_bytes=64)
        nc.vector.tensor_copy(dw_g[:], picked(dw_win[:].bitcast(U32), k1_t, ALL))

        prod = sb.tile([P, 2, PACK, S], F32, name="prod", tag="dw", align_bytes=64)
        z_pl = sb.tile([P, PACK, S], BF16, name="z_pl")
        dw_dealt = sb.tile([P, H], U32, name="dw_dealt", align_bytes=64)

        def z_tile(t):
            nc.vector.scalar_tensor_tensor(z_pl[:, t, :], prod[:, 1, t, :], coef[:, t : t + 1], prod[:, 0, t, :], ALU.mult, ALU.add)

        for t in range(PACK):
            y_out(1, t)
            g2 = sb.tile([P, S], F32, name=f"g2_{t}")
            g1 = sb.tile([P, S], F32, name=f"g1_{t}")
            nc.scalar.activation(g2[:], picked(rows[t][:], n2_t, ALL), ACT.Copy)
            nc.scalar.activation(g1[:], picked(rows[t][:], n1_t, ALL), ACT.Copy)
            nc.vector.tensor_tensor(prod[:, 1, t, :], picked(rows[t][:], n3_t, ALL), g2[:], ALU.mult)
            if t == 0:
                nc.vector.tensor_copy(
                    dw_dealt[:].rearrange("p (t c i) -> p c t i", t=PACK, i=4),
                    dw_g[:].rearrange("p (c i t) -> p c t i", t=PACK, i=4),
                )
            else:
                z_tile(t - 1)
            nc.vector.scalar_tensor_tensor(prod[:, 0, t, :], g1[:], coef[:, t : t + 1], rows[t][:, ALL], ALU.mult, ALU.mult)
        z_tile(PACK - 1)

        h_ps = [psum.tile([P, S], F32, name=f"h_ps{t}") for t in range(PACK)]
        z_bf = sb.tile([P, S * PACK], BF16, name="z_bf", align_bytes=64)
        z_to = z_bf[:].rearrange("p (c i t) -> p c t i", t=PACK, i=4)
        z_from = z_pl[:].rearrange("p t (c i) -> p c t i", i=4)
        nc.vector.tensor_copy(z_to[:, 0:96], z_from[:, 0:96])
        nc.scalar.copy(z_to[:, 96:128], z_from[:, 96:128])
        z_codes = sb.tile([P, S], U32, name="z_codes", align_bytes=64)
        z_scales = sb.tile([P, S], U8, name="z_scales", align_bytes=64)
        nc.vector.quantize_mx(out=z_codes[:].bitcast(FP8X4), scales=z_scales[:], in_=z_bf[:])
        for t in range(PACK):
            nc.tensor.matmul_mx(
                out=h_ps[t][:],
                lhsT=dw_dealt[:, P * t : P * (t + 1)].bitcast(FP8X4),
                lhsT_scale=ds_dealt[:, P * t : P * (t + 1)],
                rhs=z_codes[:].bitcast(FP8X4),
                rhs_scale=z_scales[:],
                start=True,
                stop=True,
            )

        out_rows = out.rearrange("(p t) n -> p t n", t=PACK)

        def tanh_out(t):
            nc.scalar.activation(rows[t][:, ALL], h_ps[t][:], ACT.Tanh, scale=0.03125)

        g4 = [sb.tile([P, S], F32, name=f"g4_{t}") for t in range(PACK)]
        g5 = [sb.tile([P, S], F32, name=f"g5_{t}") for t in range(PACK)]
        res = [sb.tile([P, S], F32, name=f"res{t}") for t in range(PACK)]

        def gate_on_scalar(t, cols):
            nc.scalar.activation(g4[t][:, cols], picked(rows[t][:], n4_t, cols), ACT.Copy, bias=0.03125, scale=0.03125)

        def gate_on_vector(t, cols):
            nc.vector.tensor_scalar(g4[t][:, cols], picked(rows[t][:], n4_t, cols), 0.03125, 0.03125, ALU.mult, ALU.add)

        def st_tile(t):
            nc.vector.tensor_tensor(rows[t][:, ALL], g4[t][:], h_ps[t][:], ALU.mult)

        def subtract_and_store(engine, t, cols):
            engine.tensor_tensor(res[t][:, cols], rows[t][:, cols], g5[t][:, cols], ALU.subtract)
            nc.sync.dma_start(out_rows[:, t, cols], res[t][:, cols])

        for t in (0, 1):
            tanh_out(t)
            gate_on_scalar(t, HALVES[0])
            gate_on_vector(t, HALVES[1])
            st_tile(t)
        for t in (2, 3):
            tanh_out(t)
            gate_on_scalar(t, ALL)
            st_tile(t)
        for t in (0, 1):
            nc.vector.tensor_copy(g5[t][:], picked(rows[t][:], n5_t, ALL))
            subtract_and_store(nc.gpsimd, t, ALL)
        nc.scalar.activation(g5[2][:], picked(rows[2][:], n5_t, ALL), ACT.Copy)
        nc.vector.tensor_copy(g5[3][:, HALVES[0]], picked(rows[3][:], n5_t, HALVES[0]))
        nc.scalar.activation(g5[3][:, HALVES[1]], picked(rows[3][:], n5_t, HALVES[1]), ACT.Copy)
        subtract_and_store(nc.vector, 2, ALL)
        for cols in HALVES:
            subtract_and_store(nc.vector, 3, cols)
